import numpy as np
import ml_dtypes


def mxq(x, axis, fmt="e4m3"):
    dtype, down = {"e4m3": (ml_dtypes.float8_e4m3fn, 7), "e5m2": (ml_dtypes.float8_e5m2, 14)}[fmt]
    v = np.moveaxis(np.asarray(x, np.float32).astype(ml_dtypes.bfloat16).astype(np.float64), axis, -1)
    blocks = v.reshape(v.shape[:-1] + (-1, 32))
    amax = np.abs(blocks).max(-1, keepdims=True)
    byte = np.maximum(np.where(amax > 0, np.frexp(amax)[1] - 1 + 127, 0) - down, 1)
    scale = np.exp2(byte - 127.0)
    codes = (blocks / scale).astype(np.float32).astype(dtype).astype(np.float64)
    return np.moveaxis((codes * scale).reshape(v.shape), -1, axis)


WIDE = False


def mx_kscale(k):
    if not WIDE:
        return np.ones(k)
    levels = np.array([10, -10, 5, -5, 0])
    if k % 512:
        return np.exp2(np.random.permutation(np.resize(levels, k // 32))).repeat(32)
    a = np.empty((k // 512, 16))
    for p in range(k // 512):
        a[p, :8] = np.random.permutation(np.resize(levels, 8))
        for g in range(8):
            far = levels[np.abs(levels - a[p, g]) >= 10]
            a[p, g + 8] = far[np.random.randint(len(far))]
    return np.exp2(a.ravel()).repeat(32)


BF16 = ml_dtypes.bfloat16


def bf(x):
    return np.asarray(x, np.float32).astype(BF16)


def f64(x):
    return np.asarray(x).astype(np.float64)


B, T, R, G, E, K = 2, 1024, 512, 512, 512, 1024
G2 = 2 * G
DILATION = 4


def draw0():
    s, u, t = mx_kscale(R), mx_kscale(E), mx_kscale(G)
    return {
        "x": bf(np.random.standard_normal((B, T, R)) * s),
        "cond": bf(np.random.standard_normal((B, T, E)) * u),
        "w0": bf(np.random.standard_normal((R, G2)) * (0.8 / np.sqrt(R)) / s[:, None]),
        "w1": bf(np.random.standard_normal((R, G2)) * (0.8 / np.sqrt(R)) / s[:, None]),
        "wc": bf(np.random.standard_normal((E, G2)) * (0.8 / np.sqrt(E)) / u[:, None]),
        "g": bf((1.0 + 0.1 * np.random.standard_normal(G)) * t),
        "wk": bf(np.random.standard_normal((G, K)) * (2.0 / np.sqrt(G)) / t[:, None]),
    }


def causal_delay(x, steps):
    xd = np.zeros_like(x)
    xd[:, steps:, :] = x[:, :-steps, :]
    return xd


def sigmoid(v):
    return 1.0 / (1.0 + np.exp(-v))


def core(x, cond, w0, w1, wc, g, wk):
    xq = mxq(f64(x), 2, "e4m3")
    xd = causal_delay(xq, DILATION)
    a = (xd @ mxq(f64(w0), 0, "e4m3")) + (xq @ mxq(f64(w1), 0, "e4m3")) + (mxq(f64(cond), 2, "e4m3") @ mxq(f64(wc), 0, "e4m3"))
    half = g.shape[0]
    f = a[..., :half]
    s = a[..., half:]
    z = np.tanh(f) * sigmoid(s)
    zg = z * f64(g)
    return mxq(zg, 2, "e4m3") @ mxq(f64(wk), 0, "e4m3")


def e4m3fn_bytes(y):
    return np.clip(np.asarray(y, np.float64), -448.0, 448.0).astype(np.float32).astype(ml_dtypes.float8_e4m3fn).view(np.uint8)


def e4m3fn_values(b):
    return np.asarray(b, np.uint8).view(ml_dtypes.float8_e4m3fn).astype(np.float64)


def setup_inputs():
    d = draw0()
    x0 = np.asarray(d['x']).astype(np.float64)
    s = (np.max(np.abs(x0), axis=(0, 1), keepdims=True) / 448.0).astype(np.float32)
    out = {}
    for k, v in d.items():
        if k == 'x':
            out['x_bytes'] = e4m3fn_bytes(x0 / s.astype(np.float64))
            out['x_scale'] = s
        else:
            out[k] = v
    return out


def reference(x_bytes, x_scale, cond, w0, w1, wc, g, wk):
    return core(e4m3fn_values(x_bytes) * x_scale.astype(np.float64), cond, w0, w1, wc, g, wk)

@@ -1,0 +1,348 @@
+from contextlib import ExitStack
+
+import concourse.mybir as mybir
+from concourse.masks import make_identity
+
+F32 = mybir.dt.float32
+BF16 = mybir.dt.bfloat16
+U32 = mybir.dt.uint32
+I32 = mybir.dt.int32
+U8 = mybir.dt.uint8
+FP8 = mybir.dt.float8_e4m3fn
+FP8X4 = mybir.dt.float8_e4m3fn_x4
+MULT = mybir.AluOpType.mult
+TANH = mybir.ActivationFunctionType.Tanh
+SIGMOID = mybir.ActivationFunctionType.Sigmoid
+
+P = 128
+B, T, K = 2, 1024, 512
+CH = 512
+N_OUT = 1024
+DELAY = 4
+TB = 512
+BLOCKS = B * T // TB
+RG = TB // P
+
+FLOPS = 2 * B * T * K * (3 * 2 * CH + N_OUT)
+
+
+def tile_wavenetconditionedgatelayer_kernel(tc, x_bytes, x_scale, cond, w0, w1, wc, g, wk, out):
+    nc = tc.nc
+    x_hbm = x_bytes.rearrange("b (q r p) k -> (b q) p r k", q=T // TB, p=P)
+    c_hbm = cond.rearrange("b (q r p) k -> (b q) p r k", q=T // TB, p=P)
+    out_hbm = out.rearrange("b (q r p) n -> (b q) r p n", q=T // TB, p=P)
+
+    with ExitStack() as ctx:
+        keep = ctx.enter_context(tc.tile_pool(name="keep", bufs=1))
+        work = ctx.enter_context(tc.tile_pool(name="work", bufs=2))
+        turn = ctx.enter_context(tc.psum_pool(name="psum", bufs=8))
+        acc_pool = turn
+
+        ident = keep.tile([P, P], F32, name="ident")
+        make_identity(nc, ident[:])
+        ident_bf = keep.tile([P, P], BF16, name="ident_bf")
+        nc.gpsimd.tensor_copy(out=ident_bf[:], in_=ident[:])
+        warm = keep.tile([P, 1], F32, name="warm")
+        scale_col = keep.tile([P, 4], F32, name="scale_col")
+        nc.scalar.dma_start(out=scale_col[:], in_=x_scale.rearrange("a b (p j) -> p (a b j)", j=4))
+        g_raw = keep.tile([P, 4], BF16, name="g_raw")
+        nc.scalar.dma_start(out=g_raw[:], in_=g.rearrange("(p t) -> p t", t=4))
+        nc.vector.memset(warm[:], 0.0)
+        nc.scalar.activation(out=warm[:], in_=warm[:], func=SIGMOID)
+
+        x_raw = [keep.tile([P, RG, K], U8, name="x_raw%d" % b) for b in range(BLOCKS)]
+        c_raw = [keep.tile([P, RG, K], BF16, name="c_raw%d" % b) for b in range(BLOCKS)]
+        w_raw = {}
+        w_hbm = {"w1": w1, "wc": wc, "w0": w0, "wk": wk}
+
+        def load_x(b):
+            nc.sync.dma_start(out=x_raw[b][:], in_=x_hbm[b])
+
+        def load_c(b):
+            nc.sync.dma_start(out=c_raw[b][:], in_=c_hbm[b])
+
+        for name in ("w1", "wc", "w0", "wk"):
+            for h in range(2):
+                w_raw[name, h] = keep.tile([P, 4, CH], BF16, name="raw_%s_%d" % (name, h))
+
+        def load_w(name, h):
+            src = w_hbm[name].rearrange("(p j) c -> p j c", j=4)
+            nc.sync.dma_start(out=w_raw[name, h][:], in_=src[:, :, h * CH : (h + 1) * CH])
+
+        load_x(0)
+        load_w("w1", 0)
+        load_w("w1", 1)
+        load_c(0)
+        load_w("wc", 0)
+        load_w("wc", 1)
+        load_x(1)
+        load_w("w0", 0)
+        load_w("w0", 1)
+        load_c(1)
+        load_w("wk", 0)
+        load_w("wk", 1)
+        for b in range(2, BLOCKS):
+            load_x(b)
+            load_c(b)
+
+        w_codes, w_scales = {}, {}
+        for name in ("w1", "wc", "w0", "wk"):
+            for h in range(2):
+                w_codes[name, h] = keep.tile([P, CH], U32, name="codes_%s_%d" % (name, h), align_bytes=64)
+                w_scales[name, h] = keep.tile([P, CH], U8, name="scales_%s_%d" % (name, h), align_bytes=64)
+        xq = [keep.tile([P, T], U32, name="xq%d" % i, align_bytes=64) for i in range(B)]
+        xq_s = [keep.tile([P, T], U8, name="xqs%d" % i, align_bytes=64) for i in range(B)]
+        xd = [keep.tile([P, T], U32, name="xd%d" % i, align_bytes=64) for i in range(B)]
+        xd_s = [keep.tile([P, T], U8, name="xds%d" % i, align_bytes=64) for i in range(B)]
+        for i in range(B):
+            nc.vector.memset(xd[i][:, 0:DELAY], 0)
+            nc.vector.memset(xd_s[i][:, 0:DELAY].bitcast(I32), 0)
+
+        g_col = keep.tile([P, 4], F32, name="g_col")
+        nc.vector.tensor_copy(out=g_col[:], in_=g_raw[:])
+
+        w_group = {}
+
+        def interleave_w(engine, name, h, part=None):
+            raw = w_raw[name, h]
+            if part in (None, 0):
+                w_group[name, h] = work.tile([P, CH * 4], BF16, name="w_group", bufs=4, align_bytes=64)
+            dst = w_group[name, h]
+            if name == "wk":
+                d = dst[:].rearrange("p (c j) -> p c j", j=4)
+                s = raw[:].rearrange("p j c -> p c j")
+                lo, hi = (0, CH) if part is None else (part * CH // 2, (part + 1) * CH // 2)
+            else:
+                d = dst[:].rearrange("p (t m j) -> p t m j", t=4, j=4)
+                s = raw[:].rearrange("p j (m t) -> p t m j", t=4)
+                lo, hi = (0, 4) if part is None else (2 * part, 2 * part + 2)
+            if engine is nc.vector:
+                nc.vector.tensor_copy(out=d[:, lo:hi], in_=s[:, lo:hi])
+            else:
+                nc.scalar.copy(out=d[:, lo:hi], in_=s[:, lo:hi])
+
+        def interleave_w_pe(name, h, half, engine):
+            if half == 0:
+                w_group[name, h] = work.tile([P, CH * 4], BF16, name="w_group", bufs=4, align_bytes=64)
+            bank = turn.tile([P, 2, P, 4], BF16, name="bank")
+            for i in range(2):
+                nc.tensor.matmul(
+                    bank[:, i],
+                    ident_bf[:],
+                    w_raw[name, h][:, :, 2 * half + i :: 4].rearrange("p j m -> p m j"),
+                    start=True,
+                    stop=True,
+                )
+            dst = w_group[name, h][:, half * 1024 : (half + 1) * 1024]
+            if engine is nc.vector:
+                nc.vector.tensor_copy(out=dst, in_=bank[:].rearrange("p i m j -> p (i m j)"))
+            else:
+                nc.scalar.copy(out=dst, in_=bank[:].rearrange("p i m j -> p (i m j)"))
+
+        def quantize_w(name, h):
+            nc.vector.quantize_mx(out=w_codes[name, h][:].bitcast(FP8X4), scales=w_scales[name, h][:], in_=w_group[name, h][:])
+
+        scale_row = keep.tile([P, K], F32, name="scale_row")
+
+        def spread_scale():
+            bank = turn.tile([P, 4, P], F32, name="bank")
+            for j in range(4):
+                nc.tensor.transpose(bank[:, j, :], scale_col[:, j : j + 1].to_broadcast([P, P]), ident[:])
+            nc.scalar.copy(out=scale_row[:].rearrange("p (n j) -> p n j", j=4), in_=bank[:].rearrange("p j n -> p n j"))
+
+        x_bf = {}
+        grouped = {}
+
+        def scale_x(b, r):
+            if r == 0:
+                x_bf[b] = work.tile([P, RG, K], BF16, name="x_bf")
+            nc.vector.tensor_tensor(out=x_bf[b][:, r, :], in0=x_raw[b][:, r, :].bitcast(FP8), in1=scale_row[:], op=MULT)
+
+        def turn_half(kind, b, half):
+            src = x_bf[b] if kind == "x" else c_raw[b]
+            if half == 0:
+                grouped[kind, b] = work.tile([P, TB * 4], BF16, name="grouped_" + kind, align_bytes=64)
+            bank = turn.tile([P, 2, 256], F32, name="bank")
+            for i in range(2):
+                words = src[:, 2 * half + i, :].bitcast(F32)
+                for u in range(2):
+                    nc.tensor.transpose(bank[:, u, i * P : (i + 1) * P], words[:, u::2], ident[:])
+            return bank
+
+        def empty_half(engine, kind, b, half, bank):
+            dst = grouped[kind, b][:].bitcast(F32).rearrange("p (r u) -> p r u", u=2)[:, half * 256 : (half + 1) * 256]
+            src = bank[:].rearrange("p u r -> p r u")
+            if engine is nc.vector:
+                nc.vector.tensor_copy(out=dst, in_=src)
+            else:
+                nc.scalar.copy(out=dst, in_=src)
+
+        cq = [keep.tile([P, TB], U32, name="cq%d" % b, align_bytes=64) for b in range(BLOCKS)]
+        cq_s = [keep.tile([P, TB], U8, name="cqs%d" % b, align_bytes=64) for b in range(BLOCKS)]
+
+        def quantize_x(b):
+            i, lo = b // 2, (b % 2) * TB
+            nc.vector.quantize_mx(out=xq[i][:, lo : lo + TB].bitcast(FP8X4), scales=xq_s[i][:, lo : lo + TB], in_=grouped["x", b][:])
+
+        def delay_x(b):
+            i = b // 2
+            lo, hi = (DELAY, TB) if b % 2 == 0 else (TB, T)
+            nc.vector.tensor_copy(out=xd[i][:, lo:hi].bitcast(I32), in_=xq[i][:, lo - DELAY : hi - DELAY].bitcast(I32))
+            nc.vector.tensor_copy(out=xd_s[i][:, lo:hi].bitcast(I32), in_=xq_s[i][:, lo - DELAY : hi - DELAY].bitcast(I32))
+
+        def quantize_c(b):
+            nc.vector.quantize_mx(out=cq[b][:].bitcast(FP8X4), scales=cq_s[b][:], in_=grouped["c", b][:])
+
+        acc = {}
+
+        def moving(name, c):
+            b, lo, hi = c
+            i, at = b // 2, (b % 2) * TB
+            if name == "w1":
+                return xq[i][:, at + lo : at + hi], xq_s[i][:, at + lo : at + hi]
+            if name == "w0":
+                return xd[i][:, at + lo : at + hi], xd_s[i][:, at + lo : at + hi]
+            return cq[b][:, lo:hi], cq_s[b][:, lo:hi]
+
+        def gate_pass(b, h, t, name):
+            if name == "w1":
+                acc[b, h, t] = acc_pool.tile([P, b[2] - b[1]], F32, name="bank")
+            codes, scales = moving(name, b)
+            cols = slice(t * P, (t + 1) * P)
+            nc.tensor.matmul_mx(
+                out=acc[b, h, t][:],
+                lhsT=w_codes[name, h][:, cols].bitcast(FP8X4),
+                lhsT_scale=w_scales[name, h][:, cols],
+                rhs=codes.bitcast(FP8X4),
+                rhs_scale=scales,
+                start=(name == "w1"),
+                stop=(name == "w0"),
+            )
+
+        gate = {}
+
+        def activate(b, h, t):
+            if (b, h) not in gate:
+                gate[b, h] = work.tile([P, 4, b[2] - b[1]], F32, name="tanh_f" if h == 0 else "sig_s")
+            nc.scalar.activation(out=gate[b, h][:, t, :], in_=acc[b, h, t][:], func=TANH if h == 0 else SIGMOID)
+
+        z, z_group, zq, zq_s = {}, {}, {}, {}
+
+        def combine(b, t):
+            if t == 0:
+                z[b] = work.tile([P, 4, b[2] - b[1]], BF16, name="z")
+            nc.vector.scalar_tensor_tensor(
+                out=z[b][:, t, :], in0=gate[b, 0][:, t, :], scalar=g_col[:, t : t + 1], in1=gate[b, 1][:, t, :], op0=MULT, op1=MULT
+            )
+
+        def interleave_z(b):
+            z_group[b] = work.tile([P, (b[2] - b[1]) * 4], BF16, name="z_group", align_bytes=64)
+            nc.vector.tensor_copy(out=z_group[b][:].rearrange("p (c t) -> p c t", t=4), in_=z[b][:].rearrange("p t c -> p c t"))
+
+        def quantize_z(b):
+            zq[b] = work.tile([P, b[2] - b[1]], U32, name="zq", bufs=3, align_bytes=64)
+            zq_s[b] = work.tile([P, b[2] - b[1]], U8, name="zq_s", bufs=3, align_bytes=64)
+            nc.vector.quantize_mx(out=zq[b][:].bitcast(FP8X4), scales=zq_s[b][:], in_=z_group[b][:])
+
+        o_tile = {}
+
+        def out_pass(b, r, n):
+            acc["o", b, r, n] = acc_pool.tile([P, TB], F32, name="bank")
+            cols = slice(r * P, (r + 1) * P)
+            nc.tensor.matmul_mx(
+                out=acc["o", b, r, n][:],
+                lhsT=zq[b][:, cols].bitcast(FP8X4),
+                lhsT_scale=zq_s[b][:, cols],
+                rhs=w_codes["wk", n][:].bitcast(FP8X4),
+                rhs_scale=w_scales["wk", n][:],
+                start=True,
+                stop=True,
+            )
+
+        def out_copy(engine, b, r, n):
+            if n == 0:
+                o_tile[b, r] = work.tile([P, N_OUT], F32, name="o_tile", bufs=4)
+            dst = o_tile[b, r][:, n * TB : (n + 1) * TB]
+            if engine is nc.vector:
+                nc.vector.tensor_copy(out=dst, in_=acc["o", b, r, n][:])
+            else:
+                nc.scalar.copy(out=dst, in_=acc["o", b, r, n][:])
+
+        def store(b, r):
+            nc.sync.dma_start(out=out_hbm[b[0], b[1] // P + r], in_=o_tile[b, r][:])
+
+        V, S = nc.vector, nc.scalar
+
+        def prepare(kind, b, engines=(S, S)):
+            for half in range(2):
+                if kind == "x":
+                    scale_x(b, 2 * half)
+                    scale_x(b, 2 * half + 1)
+                bank = turn_half(kind, b, half)
+                empty_half(engines[half], kind, b, half, bank)
+            if kind == "x":
+                quantize_x(b)
+            else:
+                quantize_c(b)
+
+        def run_group(b, t, names=("w1", "wc", "w0")):
+            for h in range(2):
+                for name in names:
+                    gate_pass(b, h, t, name)
+            if names[-1] == "w0":
+                for h in range(2):
+                    activate(b, h, t)
+
+        def second(b, r, engines):
+            for n in range(2):
+                out_pass(b, r, n)
+                out_copy(engines[n], b, r, n)
+            store(b, r)
+
+        spread_scale()
+        prepare("x", 0)
+        for name in ("w1", "wc", "w0"):
+            if name in ("w1",):
+                for h in range(2):
+                    interleave_w_pe(name, h, 0, S)
+                    interleave_w_pe(name, h, 1, S)
+                    quantize_w(name, h)
+            else:
+                interleave_w(V, name, 0)
+                quantize_w(name, 0)
+                interleave_w(S, name, 1, 0)
+                interleave_w(S, name, 1, 1)
+                quantize_w(name, 1)
+            if name == "w1":
+                prepare("c", 0)
+        delay_x(0)
+        chunks = [(0, 0, 512), (1, 0, 512), (2, 0, 512), (3, 0, 256), (3, 256, 512)]
+        todo = []
+        k = 0
+
+        def second_some(n):
+            for q in range(n):
+                if todo:
+                    second(*todo.pop(0), (S, V))
+
+        sched = [0]*7+[1]*20
+        for c in chunks:
+            if c[1] == 0 and c[0] + 1 < BLOCKS:
+                prepare("x", c[0] + 1)
+                prepare("c", c[0] + 1)
+                delay_x(c[0] + 1)
+            for t in range(4):
+                run_group(c, t)
+                combine(c, t)
+                if k == 5:
+                    interleave_w(V, "wk", 0)
+                    quantize_w("wk", 0)
+                    interleave_w(S, "wk", 1, 0)
+                    interleave_w(S, "wk", 1, 1)
+                    quantize_w("wk", 1)
+                second_some(sched[k] if k < len(sched) else 1)
+                k += 1
+            interleave_z(c)
+            quantize_z(c)
+            todo += [(c, r) for r in range((c[2] - c[1]) // P)]
+        second_some(100)

@@ -35,9 +35,9 @@ def tile_wavenetconditionedgatelayer_kernel(tc, x_bytes, x_scale, cond, w0, w1, 
     with ExitStack() as ctx:
         keep = ctx.enter_context(tc.tile_pool(name="keep", bufs=1))
         work = ctx.enter_context(tc.tile_pool(name="work", bufs=2))
-        turn = ctx.enter_context(tc.psum_pool(name="psum", bufs=8))
-        acc_pool = turn
+        psum = ctx.enter_context(tc.psum_pool(name="psum", bufs=8))
 
+        ctx.enter_context(tc.manual_schedule())
         ident = keep.tile([P, P], F32, name="ident")
         make_identity(nc, ident[:])
         ident_bf = keep.tile([P, P], BF16, name="ident_bf")
@@ -69,21 +69,6 @@ def tile_wavenetconditionedgatelayer_kernel(tc, x_bytes, x_scale, cond, w0, w1, 
             src = w_hbm[name].rearrange("(p j) c -> p j c", j=4)
             nc.sync.dma_start(out=w_raw[name, h][:], in_=src[:, :, h * CH : (h + 1) * CH])
 
-        load_x(0)
-        load_w("w1", 0)
-        load_w("w1", 1)
-        load_c(0)
-        load_w("wc", 0)
-        load_w("wc", 1)
-        load_x(1)
-        load_w("w0", 0)
-        load_w("w0", 1)
-        load_c(1)
-        load_w("wk", 0)
-        load_w("wk", 1)
-        for b in range(2, BLOCKS):
-            load_x(b)
-            load_c(b)
 
         w_codes, w_scales = {}, {}
         for name in ("w1", "wc", "w0", "wk"):
@@ -124,7 +109,7 @@ def tile_wavenetconditionedgatelayer_kernel(tc, x_bytes, x_scale, cond, w0, w1, 
         def interleave_w_pe(name, h, half, engine):
             if half == 0:
                 w_group[name, h] = work.tile([P, CH * 4], BF16, name="w_group", bufs=4, align_bytes=64)
-            bank = turn.tile([P, 2, P, 4], BF16, name="bank")
+            bank = psum.tile([P, 2, P, 4], BF16, name="bank")
             for i in range(2):
                 nc.tensor.matmul(
                     bank[:, i],
@@ -145,7 +130,7 @@ def tile_wavenetconditionedgatelayer_kernel(tc, x_bytes, x_scale, cond, w0, w1, 
         scale_row = keep.tile([P, K], F32, name="scale_row")
 
         def spread_scale():
-            bank = turn.tile([P, 4, P], F32, name="bank")
+            bank = psum.tile([P, 4, P], F32, name="bank")
             for j in range(4):
                 nc.tensor.transpose(bank[:, j, :], scale_col[:, j : j + 1].to_broadcast([P, P]), ident[:])
             nc.scalar.copy(out=scale_row[:].rearrange("p (n j) -> p n j", j=4), in_=bank[:].rearrange("p j n -> p n j"))
@@ -155,14 +140,14 @@ def tile_wavenetconditionedgatelayer_kernel(tc, x_bytes, x_scale, cond, w0, w1, 
 
         def scale_x(b, r):
             if r == 0:
-                x_bf[b] = work.tile([P, RG, K], BF16, name="x_bf")
+                x_bf[b] = work.tile([P, RG, K], BF16, name="x_bf", bufs=3)
             nc.vector.tensor_tensor(out=x_bf[b][:, r, :], in0=x_raw[b][:, r, :].bitcast(FP8), in1=scale_row[:], op=MULT)
 
         def turn_half(kind, b, half):
             src = x_bf[b] if kind == "x" else c_raw[b]
             if half == 0:
-                grouped[kind, b] = work.tile([P, TB * 4], BF16, name="grouped_" + kind, align_bytes=64)
-            bank = turn.tile([P, 2, 256], F32, name="bank")
+                grouped[kind, b] = work.tile([P, TB * 4], BF16, name="grouped_" + kind, bufs=3 if kind == "x" else 2, align_bytes=64)
+            bank = psum.tile([P, 2, 256], F32, name="bank")
             for i in range(2):
                 words = src[:, 2 * half + i, :].bitcast(F32)
                 for u in range(2):
@@ -187,8 +172,12 @@ def tile_wavenetconditionedgatelayer_kernel(tc, x_bytes, x_scale, cond, w0, w1, 
         def delay_x(b):
             i = b // 2
             lo, hi = (DELAY, TB) if b % 2 == 0 else (TB, T)
-            nc.vector.tensor_copy(out=xd[i][:, lo:hi].bitcast(I32), in_=xq[i][:, lo - DELAY : hi - DELAY].bitcast(I32))
-            nc.vector.tensor_copy(out=xd_s[i][:, lo:hi].bitcast(I32), in_=xq_s[i][:, lo - DELAY : hi - DELAY].bitcast(I32))
+            for dst, src in ((xd[i], xq[i]), (xd_s[i], xq_s[i])):
+                moved, source = dst[:, lo:hi].bitcast(I32), src[:, lo - DELAY : hi - DELAY].bitcast(I32)
+                if b < 2:
+                    nc.vector.tensor_copy(out=moved, in_=source)
+                else:
+                    nc.sync.dma_start(out=moved, in_=source)
 
         def quantize_c(b):
             nc.vector.quantize_mx(out=cq[b][:].bitcast(FP8X4), scales=cq_s[b][:], in_=grouped["c", b][:])
@@ -206,7 +195,7 @@ def tile_wavenetconditionedgatelayer_kernel(tc, x_bytes, x_scale, cond, w0, w1, 
 
         def gate_pass(b, h, t, name):
             if name == "w1":
-                acc[b, h, t] = acc_pool.tile([P, b[2] - b[1]], F32, name="bank")
+                acc[b, h, t] = psum.tile([P, b[2] - b[1]], F32, name="bank")
             codes, scales = moving(name, b)
             cols = slice(t * P, (t + 1) * P)
             nc.tensor.matmul_mx(
@@ -247,7 +236,7 @@ def tile_wavenetconditionedgatelayer_kernel(tc, x_bytes, x_scale, cond, w0, w1, 
         o_tile = {}
 
         def out_pass(b, r, n):
-            acc["o", b, r, n] = acc_pool.tile([P, TB], F32, name="bank")
+            acc["o", b, r, n] = psum.tile([P, TB], F32, name="bank")
             cols = slice(r * P, (r + 1) * P)
             nc.tensor.matmul_mx(
                 out=acc["o", b, r, n][:],
@@ -271,78 +260,237 @@ def tile_wavenetconditionedgatelayer_kernel(tc, x_bytes, x_scale, cond, w0, w1, 
         def store(b, r):
             nc.sync.dma_start(out=out_hbm[b[0], b[1] // P + r], in_=o_tile[b, r][:])
 
+        def store_half(b, r, n):
+            cols = slice(n * TB, (n + 1) * TB)
+            nc.sync.dma_start(out=out_hbm[b[0], b[1] // P + r][:, cols], in_=o_tile[b, r][:, cols])
+
         V, S = nc.vector, nc.scalar
 
-        def prepare(kind, b, engines=(S, S)):
+        blocks = [(b, 0, TB) for b in range(BLOCKS)]
+
+        def il(name, h, first, second_half):
+            interleave_w(first, name, h, 0)
+            interleave_w(second_half, name, h, 1)
+
+        def turn(kind, b, engines=(S, S)):
             for half in range(2):
-                if kind == "x":
-                    scale_x(b, 2 * half)
-                    scale_x(b, 2 * half + 1)
                 bank = turn_half(kind, b, half)
                 empty_half(engines[half], kind, b, half, bank)
-            if kind == "x":
-                quantize_x(b)
-            else:
-                quantize_c(b)
 
-        def run_group(b, t, names=("w1", "wc", "w0")):
-            for h in range(2):
-                for name in names:
-                    gate_pass(b, h, t, name)
-            if names[-1] == "w0":
-                for h in range(2):
-                    activate(b, h, t)
+        def scale(b):
+            for r in range(RG):
+                scale_x(b, r)
+
+        def group(c, h, t):
+            for name in ("w1", "wc", "w0"):
+                gate_pass(c, h, t, name)
+            activate(c, h, t)
+
+        def finish_z(c):
+            interleave_z(c)
+            quantize_z(c)
 
         def second(b, r, engines):
             for n in range(2):
                 out_pass(b, r, n)
                 out_copy(engines[n], b, r, n)
-            store(b, r)
+                if b[2] - b[1] < TB:
+                    store_half(b, r, n)
+            if b[2] - b[1] == TB:
+                store(b, r)
 
+        load_x(0)
         spread_scale()
-        prepare("x", 0)
-        for name in ("w1", "wc", "w0"):
-            if name in ("w1",):
-                for h in range(2):
-                    interleave_w_pe(name, h, 0, S)
-                    interleave_w_pe(name, h, 1, S)
-                    quantize_w(name, h)
-            else:
-                interleave_w(V, name, 0)
-                quantize_w(name, 0)
-                interleave_w(S, name, 1, 0)
-                interleave_w(S, name, 1, 1)
-                quantize_w(name, 1)
-            if name == "w1":
-                prepare("c", 0)
+        load_w("w1", 1)
+        interleave_w(S, "w1", 1, 0)
+        load_x(1)
+        scale_x(0, 0)
+        scale_x(0, 1)
+        scale_x(0, 2)
+        scale_x(0, 3)
+        scale_x(1, 0)
+        scale_x(1, 1)
+        load_c(0)
+        interleave_w(S, "w1", 1, 1)
+        load_c(1)
+        empty_half(V, "x", 0, 0, turn_half("x", 0, 0))
+        empty_half(S, "x", 0, 1, turn_half("x", 0, 1))
+        empty_half(S, "c", 0, 0, turn_half("c", 0, 0))
+        empty_half(S, "c", 0, 1, turn_half("c", 0, 1))
+        load_w("wc", 1)
+        load_c(2)
+        load_w("w0", 1)
+        scale_x(1, 2)
+        scale_x(1, 3)
+        load_w("wc", 0)
+        empty_half(S, "c", 1, 0, turn_half("c", 1, 0))
+        quantize_x(0)
+        empty_half(S, "x", 1, 0, turn_half("x", 1, 0))
+        load_w("w1", 0)
+        empty_half(S, "x", 1, 1, turn_half("x", 1, 1))
+        quantize_w("w1", 1)
+        empty_half(S, "c", 1, 1, turn_half("c", 1, 1))
+        interleave_w(V, "wc", 1, 0)
+        quantize_c(0)
+        quantize_x(1)
+        interleave_w(S, "wc", 1, 1)
+        gate_pass(blocks[0], 1, 0, "w1")
+        gate_pass(blocks[0], 1, 1, "w1")
+        quantize_c(1)
+        gate_pass(blocks[0], 1, 2, "w1")
+        gate_pass(blocks[0], 1, 3, "w1")
+        load_x(2)
+        quantize_w("wc", 1)
+        empty_half(S, "c", 2, 0, turn_half("c", 2, 0))
+        delay_x(1)
+        interleave_w(V, "w0", 1, 0)
+        interleave_w(S, "w0", 1, 1)
+        load_w("w0", 0)
         delay_x(0)
-        chunks = [(0, 0, 512), (1, 0, 512), (2, 0, 512), (3, 0, 256), (3, 256, 512)]
-        todo = []
-        k = 0
-
-        def second_some(n):
-            for q in range(n):
-                if todo:
-                    second(*todo.pop(0), (S, V))
-
-        sched = [0]*7+[1]*20
-        for c in chunks:
-            if c[1] == 0 and c[0] + 1 < BLOCKS:
-                prepare("x", c[0] + 1)
-                prepare("c", c[0] + 1)
-                delay_x(c[0] + 1)
-            for t in range(4):
-                run_group(c, t)
-                combine(c, t)
-                if k == 5:
-                    interleave_w(V, "wk", 0)
-                    quantize_w("wk", 0)
-                    interleave_w(S, "wk", 1, 0)
-                    interleave_w(S, "wk", 1, 1)
-                    quantize_w("wk", 1)
-                second_some(sched[k] if k < len(sched) else 1)
-                k += 1
-            interleave_z(c)
-            quantize_z(c)
-            todo += [(c, r) for r in range((c[2] - c[1]) // P)]
-        second_some(100)
+        gate_pass(blocks[1], 1, 0, "w1")
+        gate_pass(blocks[1], 1, 1, "w1")
+        load_c(3)
+        quantize_w("w0", 1)
+        gate_pass(blocks[1], 1, 2, "w1")
+        gate_pass(blocks[1], 1, 3, "w1")
+        interleave_w(V, "wc", 0, 0)
+        interleave_w(V, "w1", 0, 0)
+        gate_pass(blocks[0], 1, 0, "wc")
+        gate_pass(blocks[0], 1, 1, "wc")
+        gate_pass(blocks[1], 1, 0, "wc")
+        gate_pass(blocks[1], 1, 1, "wc")
+        load_x(3)
+        interleave_w(S, "wc", 0, 1)
+        scale_x(2, 0)
+        scale_x(2, 1)
+        interleave_w(S, "w1", 0, 1)
+        gate_pass(blocks[1], 1, 2, "wc")
+        gate_pass(blocks[1], 1, 3, "wc")
+        gate_pass(blocks[0], 1, 2, "wc")
+        gate_pass(blocks[0], 1, 3, "wc")
+        interleave_w(V, "w0", 0, 0)
+        gate_pass(blocks[0], 1, 0, "w0")
+        activate(blocks[0], 1, 0)
+        gate_pass(blocks[0], 1, 1, "w0")
+        activate(blocks[0], 1, 1)
+        gate_pass(blocks[1], 1, 0, "w0")
+        activate(blocks[1], 1, 0)
+        gate_pass(blocks[1], 1, 1, "w0")
+        activate(blocks[1], 1, 1)
+        interleave_w(V, "w0", 0, 1)
+        quantize_w("w1", 0)
+        quantize_w("wc", 0)
+        load_w("wk", 0)
+        gate_pass(blocks[0], 1, 2, "w0")
+        activate(blocks[0], 1, 2)
+        gate_pass(blocks[0], 1, 3, "w0")
+        activate(blocks[0], 1, 3)
+        empty_half(S, "c", 2, 1, turn_half("c", 2, 1))
+        empty_half(S, "c", 3, 0, turn_half("c", 3, 0))
+        load_w("wk", 1)
+        quantize_w("w0", 0)
+        scale_x(2, 2)
+        scale_x(2, 3)
+        scale_x(3, 0)
+        scale_x(3, 1)
+        empty_half(S, "x", 2, 0, turn_half("x", 2, 0))
+        gate_pass(blocks[1], 1, 2, "w0")
+        activate(blocks[1], 1, 2)
+        gate_pass(blocks[1], 1, 3, "w0")
+        activate(blocks[1], 1, 3)
+        interleave_w(V, "wk", 1, 0)
+        empty_half(V, "c", 3, 1, turn_half("c", 3, 1))
+        scale_x(3, 2)
+        scale_x(3, 3)
+        group(blocks[1], 0, 0)
+        group(blocks[0], 0, 0)
+        group(blocks[1], 0, 1)
+        empty_half(S, "x", 2, 1, turn_half("x", 2, 1))
+        empty_half(S, "x", 3, 0, turn_half("x", 3, 0))
+        quantize_x(2)
+        combine(blocks[0], 0)
+        combine(blocks[1], 0)
+        group(blocks[0], 0, 1)
+        delay_x(2)
+        combine(blocks[0], 1)
+        interleave_w(S, "wk", 1, 1)
+        group(blocks[0], 0, 2)
+        quantize_c(2)
+        empty_half(S, "x", 3, 1, turn_half("x", 3, 1))
+        group(blocks[0], 0, 3)
+        interleave_w(S, "wk", 0, 0)
+        combine(blocks[0], 2)
+        quantize_w("wk", 1)
+        group(blocks[1], 0, 2)
+        combine(blocks[0], 3)
+        combine(blocks[1], 1)
+        interleave_w(S, "wk", 0, 1)
+        group(blocks[1], 0, 3)
+        quantize_x(3)
+        delay_x(3)
+        interleave_z(blocks[0])
+        group(blocks[2], 0, 0)
+        group(blocks[2], 1, 0)
+        quantize_w("wk", 0)
+        group(blocks[2], 0, 1)
+        quantize_z(blocks[0])
+        combine(blocks[1], 2)
+        group(blocks[2], 1, 1)
+        group(blocks[2], 1, 2)
+        combine(blocks[1], 3)
+        second(blocks[0], 0, (V, S))
+        second(blocks[0], 1, (S, S))
+        interleave_z(blocks[1])
+        second(blocks[0], 2, (S, S))
+        second(blocks[0], 3, (V, V))
+        quantize_z(blocks[1])
+        group(blocks[2], 1, 3)
+        quantize_c(3)
+        group(blocks[2], 0, 2)
+        group(blocks[2], 0, 3)
+        combine(blocks[2], 0)
+        second(blocks[1], 0, (S, S))
+        combine(blocks[2], 1)
+        combine(blocks[2], 2)
+        second(blocks[1], 1, (S, S))
+        combine(blocks[2], 3)
+        group((3, 0, 256), 0, 0)
+        group((3, 0, 256), 1, 0)
+        interleave_z(blocks[2])
+        group((3, 256, 512), 1, 0)
+        second(blocks[1], 2, (V, S))
+        group((3, 0, 256), 0, 1)
+        quantize_z(blocks[2])
+        group((3, 0, 256), 1, 1)
+        combine((3, 0, 256), 0)
+        second(blocks[1], 3, (V, S))
+        group((3, 0, 256), 1, 2)
+        group((3, 0, 256), 0, 2)
+        group((3, 0, 256), 0, 3)
+        combine((3, 0, 256), 1)
+        second(blocks[2], 0, (V, V))
+        group((3, 0, 256), 1, 3)
+        combine((3, 0, 256), 2)
+        group((3, 256, 512), 0, 0)
+        second(blocks[2], 1, (S, S))
+        combine((3, 0, 256), 3)
+        group((3, 256, 512), 1, 1)
+        interleave_z((3, 0, 256))
+        group((3, 256, 512), 0, 1)
+        second(blocks[2], 2, (S, V))
+        group((3, 256, 512), 0, 2)
+        quantize_z((3, 0, 256))
+        second(blocks[2], 3, (V, S))
+        combine((3, 256, 512), 0)
+        group((3, 256, 512), 1, 2)
+        group((3, 256, 512), 1, 3)
+        group((3, 256, 512), 0, 3)
+        combine((3, 256, 512), 1)
+        second((3, 0, 256), 0, (S, S))
+        combine((3, 256, 512), 2)
+        combine((3, 256, 512), 3)
+        interleave_z((3, 256, 512))
+        second((3, 0, 256), 1, (S, S))
+        quantize_z((3, 256, 512))
+        second((3, 256, 512), 0, (S, S))
+        second((3, 256, 512), 1, (S, V))

@@ -94,13 +94,13 @@ def tile_wavenetconditionedgatelayer_kernel(tc, x_bytes, x_scale, cond, w0, w1, 
                 w_group[name, h] = work.tile([P, CH * 4], BF16, name="w_group", bufs=4, align_bytes=64)
             dst = w_group[name, h]
             if name == "wk":
-                d = dst[:].rearrange("p (c j) -> p c j", j=4)
-                s = raw[:].rearrange("p j c -> p c j")
-                lo, hi = (0, CH) if part is None else (part * CH // 2, (part + 1) * CH // 2)
+                d = dst[:].rearrange("p (c i j) -> p c j i", i=4, j=4)
+                s = raw[:].rearrange("p j (c i) -> p c j i", i=4)
+                lo, hi = (P // 2 * part, P // 2 * (part + 1))
             else:
-                d = dst[:].rearrange("p (t m j) -> p t m j", t=4, j=4)
-                s = raw[:].rearrange("p j (m t) -> p t m j", t=4)
-                lo, hi = (0, 4) if part is None else (2 * part, 2 * part + 2)
+                d = dst[:].rearrange("p (t m j) -> p m j t", t=4, j=4)
+                s = raw[:].rearrange("p j (m t) -> p m j t", t=4)
+                lo, hi = (P // 2 * part, P // 2 * (part + 1))
             if engine is nc.vector:
                 nc.vector.tensor_copy(out=d[:, lo:hi], in_=s[:, lo:hi])
             else:
@@ -226,7 +226,9 @@ def tile_wavenetconditionedgatelayer_kernel(tc, x_bytes, x_scale, cond, w0, w1, 
 
         def interleave_z(b):
             z_group[b] = work.tile([P, (b[2] - b[1]) * 4], BF16, name="z_group", align_bytes=64)
-            nc.vector.tensor_copy(out=z_group[b][:].rearrange("p (c t) -> p c t", t=4), in_=z[b][:].rearrange("p t c -> p c t"))
+            nc.vector.tensor_copy(
+                out=z_group[b][:].rearrange("p (c i t) -> p c t i", i=4, t=4), in_=z[b][:].rearrange("p t (c i) -> p c t i", i=4)
+            )
 
         def quantize_z(b):
             zq[b] = work.tile([P, b[2] - b[1]], U32, name="zq", bufs=3, align_bytes=64)

from contextlib import ExitStack

import concourse.mybir as mybir
from concourse.masks import make_identity

F32 = mybir.dt.float32
BF16 = mybir.dt.bfloat16
U32 = mybir.dt.uint32
I32 = mybir.dt.int32
U8 = mybir.dt.uint8
FP8 = mybir.dt.float8_e4m3fn
FP8X4 = mybir.dt.float8_e4m3fn_x4
MULT = mybir.AluOpType.mult
TANH = mybir.ActivationFunctionType.Tanh
SIGMOID = mybir.ActivationFunctionType.Sigmoid

P = 128
B, T, K = 2, 1024, 512
CH = 512
N_OUT = 1024
DELAY = 4
TB = 512
BLOCKS = B * T // TB
RG = TB // P

FLOPS = 2 * B * T * K * (3 * 2 * CH + N_OUT)


def tile_wavenetconditionedgatelayer_kernel(tc, x_bytes, x_scale, cond, w0, w1, wc, g, wk, out):
    nc = tc.nc
    x_hbm = x_bytes.rearrange("b (q r p) k -> (b q) p r k", q=T // TB, p=P)
    c_hbm = cond.rearrange("b (q r p) k -> (b q) p r k", q=T // TB, p=P)
    out_hbm = out.rearrange("b (q r p) n -> (b q) r p n", q=T // TB, p=P)

    with ExitStack() as ctx:
        keep = ctx.enter_context(tc.tile_pool(name="keep", bufs=1))
        work = ctx.enter_context(tc.tile_pool(name="work", bufs=2))
        psum = ctx.enter_context(tc.psum_pool(name="psum", bufs=8))

        ctx.enter_context(tc.manual_schedule())
        ident = keep.tile([P, P], F32, name="ident")
        make_identity(nc, ident[:])
        ident_bf = keep.tile([P, P], BF16, name="ident_bf")
        nc.gpsimd.tensor_copy(out=ident_bf[:], in_=ident[:])
        warm = keep.tile([P, 1], F32, name="warm")
        scale_col = keep.tile([P, 4], F32, name="scale_col")
        nc.scalar.dma_start(out=scale_col[:], in_=x_scale.rearrange("a b (p j) -> p (a b j)", j=4))
        g_raw = keep.tile([P, 4], BF16, name="g_raw")
        nc.scalar.dma_start(out=g_raw[:], in_=g.rearrange("(p t) -> p t", t=4))
        nc.vector.memset(warm[:], 0.0)
        nc.scalar.activation(out=warm[:], in_=warm[:], func=SIGMOID)

        x_raw = [keep.tile([P, RG, K], U8, name="x_raw%d" % b) for b in range(BLOCKS)]
        c_raw = [keep.tile([P, RG, K], BF16, name="c_raw%d" % b) for b in range(BLOCKS)]
        w_raw = {}
        w_hbm = {"w1": w1, "wc": wc, "w0": w0, "wk": wk}

        def load_x(b):
            nc.sync.dma_start(out=x_raw[b][:], in_=x_hbm[b])

        def load_c(b):
            nc.sync.dma_start(out=c_raw[b][:], in_=c_hbm[b])

        for name in ("w1", "wc", "w0", "wk"):
            for h in range(2):
                w_raw[name, h] = keep.tile([P, 4, CH], BF16, name="raw_%s_%d" % (name, h))

        def load_w(name, h):
            src = w_hbm[name].rearrange("(p j) c -> p j c", j=4)
            nc.sync.dma_start(out=w_raw[name, h][:], in_=src[:, :, h * CH : (h + 1) * CH])


        w_codes, w_scales = {}, {}
        for name in ("w1", "wc", "w0", "wk"):
            for h in range(2):
                w_codes[name, h] = keep.tile([P, CH], U32, name="codes_%s_%d" % (name, h), align_bytes=64)
                w_scales[name, h] = keep.tile([P, CH], U8, name="scales_%s_%d" % (name, h), align_bytes=64)
        xq = [keep.tile([P, T], U32, name="xq%d" % i, align_bytes=64) for i in range(B)]
        xq_s = [keep.tile([P, T], U8, name="xqs%d" % i, align_bytes=64) for i in range(B)]
        xd = [keep.tile([P, T], U32, name="xd%d" % i, align_bytes=64) for i in range(B)]
        xd_s = [keep.tile([P, T], U8, name="xds%d" % i, align_bytes=64) for i in range(B)]
        for i in range(B):
            nc.vector.memset(xd[i][:, 0:DELAY], 0)
            nc.vector.memset(xd_s[i][:, 0:DELAY].bitcast(I32), 0)

        g_col = keep.tile([P, 4], F32, name="g_col")
        nc.vector.tensor_copy(out=g_col[:], in_=g_raw[:])

        w_group = {}

        def interleave_w(engine, name, h, part=None):
            raw = w_raw[name, h]
            if part in (None, 0):
                w_group[name, h] = work.tile([P, CH * 4], BF16, name="w_group", bufs=4, align_bytes=64)
            dst = w_group[name, h]
            if name == "wk":
                d = dst[:].rearrange("p (c i j) -> p c j i", i=4, j=4)
                s = raw[:].rearrange("p j (c i) -> p c j i", i=4)
                lo, hi = (P // 2 * part, P // 2 * (part + 1))
            else:
                d = dst[:].rearrange("p (t m j) -> p m j t", t=4, j=4)
                s = raw[:].rearrange("p j (m t) -> p m j t", t=4)
                lo, hi = (P // 2 * part, P // 2 * (part + 1))
            if engine is nc.vector:
                nc.vector.tensor_copy(out=d[:, lo:hi], in_=s[:, lo:hi])
            else:
                nc.scalar.copy(out=d[:, lo:hi], in_=s[:, lo:hi])

        def interleave_w_pe(name, h, half, engine):
            if half == 0:
                w_group[name, h] = work.tile([P, CH * 4], BF16, name="w_group", bufs=4, align_bytes=64)
            bank = psum.tile([P, 2, P, 4], BF16, name="bank")
            for i in range(2):
                nc.tensor.matmul(
                    bank[:, i],
                    ident_bf[:],
                    w_raw[name, h][:, :, 2 * half + i :: 4].rearrange("p j m -> p m j"),
                    start=True,
                    stop=True,
                )
            dst = w_group[name, h][:, half * 1024 : (half + 1) * 1024]
            if engine is nc.vector:
                nc.vector.tensor_copy(out=dst, in_=bank[:].rearrange("p i m j -> p (i m j)"))
            else:
                nc.scalar.copy(out=dst, in_=bank[:].rearrange("p i m j -> p (i m j)"))

        def quantize_w(name, h):
            nc.vector.quantize_mx(out=w_codes[name, h][:].bitcast(FP8X4), scales=w_scales[name, h][:], in_=w_group[name, h][:])

        scale_row = keep.tile([P, K], F32, name="scale_row")

        def spread_scale():
            bank = psum.tile([P, 4, P], F32, name="bank")
            for j in range(4):
                nc.tensor.transpose(bank[:, j, :], scale_col[:, j : j + 1].to_broadcast([P, P]), ident[:])
            nc.scalar.copy(out=scale_row[:].rearrange("p (n j) -> p n j", j=4), in_=bank[:].rearrange("p j n -> p n j"))

        x_bf = {}
        grouped = {}

        def scale_x(b, r):
            if r == 0:
                x_bf[b] = work.tile([P, RG, K], BF16, name="x_bf", bufs=3)
            nc.vector.tensor_tensor(out=x_bf[b][:, r, :], in0=x_raw[b][:, r, :].bitcast(FP8), in1=scale_row[:], op=MULT)

        def turn_half(kind, b, half):
            src = x_bf[b] if kind == "x" else c_raw[b]
            if half == 0:
                grouped[kind, b] = work.tile([P, TB * 4], BF16, name="grouped_" + kind, bufs=3 if kind == "x" else 2, align_bytes=64)
            bank = psum.tile([P, 2, 256], F32, name="bank")
            for i in range(2):
                words = src[:, 2 * half + i, :].bitcast(F32)
                for u in range(2):
                    nc.tensor.transpose(bank[:, u, i * P : (i + 1) * P], words[:, u::2], ident[:])
            return bank

        def empty_half(engine, kind, b, half, bank):
            dst = grouped[kind, b][:].bitcast(F32).rearrange("p (r u) -> p r u", u=2)[:, half * 256 : (half + 1) * 256]
            src = bank[:].rearrange("p u r -> p r u")
            if engine is nc.vector:
                nc.vector.tensor_copy(out=dst, in_=src)
            else:
                nc.scalar.copy(out=dst, in_=src)

        cq = [keep.tile([P, TB], U32, name="cq%d" % b, align_bytes=64) for b in range(BLOCKS)]
        cq_s = [keep.tile([P, TB], U8, name="cqs%d" % b, align_bytes=64) for b in range(BLOCKS)]

        def quantize_x(b):
            i, lo = b // 2, (b % 2) * TB
            nc.vector.quantize_mx(out=xq[i][:, lo : lo + TB].bitcast(FP8X4), scales=xq_s[i][:, lo : lo + TB], in_=grouped["x", b][:])

        def delay_x(b):
            i = b // 2
            lo, hi = (DELAY, TB) if b % 2 == 0 else (TB, T)
            for dst, src in ((xd[i], xq[i]), (xd_s[i], xq_s[i])):
                moved, source = dst[:, lo:hi].bitcast(I32), src[:, lo - DELAY : hi - DELAY].bitcast(I32)
                if b < 2:
                    nc.vector.tensor_copy(out=moved, in_=source)
                else:
                    nc.sync.dma_start(out=moved, in_=source)

        def quantize_c(b):
            nc.vector.quantize_mx(out=cq[b][:].bitcast(FP8X4), scales=cq_s[b][:], in_=grouped["c", b][:])

        acc = {}

        def moving(name, c):
            b, lo, hi = c
            i, at = b // 2, (b % 2) * TB
            if name == "w1":
                return xq[i][:, at + lo : at + hi], xq_s[i][:, at + lo : at + hi]
            if name == "w0":
                return xd[i][:, at + lo : at + hi], xd_s[i][:, at + lo : at + hi]
            return cq[b][:, lo:hi], cq_s[b][:, lo:hi]

        def gate_pass(b, h, t, name):
            if name == "w1":
                acc[b, h, t] = psum.tile([P, b[2] - b[1]], F32, name="bank")
            codes, scales = moving(name, b)
            cols = slice(t * P, (t + 1) * P)
            nc.tensor.matmul_mx(
                out=acc[b, h, t][:],
                lhsT=w_codes[name, h][:, cols].bitcast(FP8X4),
                lhsT_scale=w_scales[name, h][:, cols],
                rhs=codes.bitcast(FP8X4),
                rhs_scale=scales,
                start=(name == "w1"),
                stop=(name == "w0"),
            )

        gate = {}

        def activate(b, h, t):
            if (b, h) not in gate:
                gate[b, h] = work.tile([P, 4, b[2] - b[1]], F32, name="tanh_f" if h == 0 else "sig_s")
            nc.scalar.activation(out=gate[b, h][:, t, :], in_=acc[b, h, t][:], func=TANH if h == 0 else SIGMOID)

        z, z_group, zq, zq_s = {}, {}, {}, {}

        def combine(b, t):
            if t == 0:
                z[b] = work.tile([P, 4, b[2] - b[1]], BF16, name="z")
            nc.vector.scalar_tensor_tensor(
                out=z[b][:, t, :], in0=gate[b, 0][:, t, :], scalar=g_col[:, t : t + 1], in1=gate[b, 1][:, t, :], op0=MULT, op1=MULT
            )

        def interleave_z(b):
            z_group[b] = work.tile([P, (b[2] - b[1]) * 4], BF16, name="z_group", align_bytes=64)
            nc.vector.tensor_copy(
                out=z_group[b][:].rearrange("p (c i t) -> p c t i", i=4, t=4), in_=z[b][:].rearrange("p t (c i) -> p c t i", i=4)
            )

        def quantize_z(b):
            zq[b] = work.tile([P, b[2] - b[1]], U32, name="zq", bufs=3, align_bytes=64)
            zq_s[b] = work.tile([P, b[2] - b[1]], U8, name="zq_s", bufs=3, align_bytes=64)
            nc.vector.quantize_mx(out=zq[b][:].bitcast(FP8X4), scales=zq_s[b][:], in_=z_group[b][:])

        o_tile = {}

        def out_pass(b, r, n):
            acc["o", b, r, n] = psum.tile([P, TB], F32, name="bank")
            cols = slice(r * P, (r + 1) * P)
            nc.tensor.matmul_mx(
                out=acc["o", b, r, n][:],
                lhsT=zq[b][:, cols].bitcast(FP8X4),
                lhsT_scale=zq_s[b][:, cols],
                rhs=w_codes["wk", n][:].bitcast(FP8X4),
                rhs_scale=w_scales["wk", n][:],
                start=True,
                stop=True,
            )

        def out_copy(engine, b, r, n):
            if n == 0:
                o_tile[b, r] = work.tile([P, N_OUT], F32, name="o_tile", bufs=4)
            dst = o_tile[b, r][:, n * TB : (n + 1) * TB]
            if engine is nc.vector:
                nc.vector.tensor_copy(out=dst, in_=acc["o", b, r, n][:])
            else:
                nc.scalar.copy(out=dst, in_=acc["o", b, r, n][:])

        def store(b, r):
            nc.sync.dma_start(out=out_hbm[b[0], b[1] // P + r], in_=o_tile[b, r][:])

        def store_half(b, r, n):
            cols = slice(n * TB, (n + 1) * TB)
            nc.sync.dma_start(out=out_hbm[b[0], b[1] // P + r][:, cols], in_=o_tile[b, r][:, cols])

        V, S = nc.vector, nc.scalar

        blocks = [(b, 0, TB) for b in range(BLOCKS)]

        def il(name, h, first, second_half):
            interleave_w(first, name, h, 0)
            interleave_w(second_half, name, h, 1)

        def turn(kind, b, engines=(S, S)):
            for half in range(2):
                bank = turn_half(kind, b, half)
                empty_half(engines[half], kind, b, half, bank)

        def scale(b):
            for r in range(RG):
                scale_x(b, r)

        def group(c, h, t):
            for name in ("w1", "wc", "w0"):
                gate_pass(c, h, t, name)
            activate(c, h, t)

        def finish_z(c):
            interleave_z(c)
            quantize_z(c)

        def second(b, r, engines):
            for n in range(2):
                out_pass(b, r, n)
                out_copy(engines[n], b, r, n)
                if b[2] - b[1] < TB:
                    store_half(b, r, n)
            if b[2] - b[1] == TB:
                store(b, r)

        load_x(0)
        spread_scale()
        load_w("w1", 1)
        interleave_w(S, "w1", 1, 0)
        load_x(1)
        scale_x(0, 0)
        scale_x(0, 1)
        scale_x(0, 2)
        scale_x(0, 3)
        scale_x(1, 0)
        scale_x(1, 1)
        load_c(0)
        interleave_w(S, "w1", 1, 1)
        load_c(1)
        empty_half(V, "x", 0, 0, turn_half("x", 0, 0))
        empty_half(S, "x", 0, 1, turn_half("x", 0, 1))
        empty_half(S, "c", 0, 0, turn_half("c", 0, 0))
        empty_half(S, "c", 0, 1, turn_half("c", 0, 1))
        load_w("wc", 1)
        load_c(2)
        load_w("w0", 1)
        scale_x(1, 2)
        scale_x(1, 3)
        load_w("wc", 0)
        empty_half(S, "c", 1, 0, turn_half("c", 1, 0))
        quantize_x(0)
        empty_half(S, "x", 1, 0, turn_half("x", 1, 0))
        load_w("w1", 0)
        empty_half(S, "x", 1, 1, turn_half("x", 1, 1))
        quantize_w("w1", 1)
        empty_half(S, "c", 1, 1, turn_half("c", 1, 1))
        interleave_w(V, "wc", 1, 0)
        quantize_c(0)
        quantize_x(1)
        interleave_w(S, "wc", 1, 1)
        gate_pass(blocks[0], 1, 0, "w1")
        gate_pass(blocks[0], 1, 1, "w1")
        quantize_c(1)
        gate_pass(blocks[0], 1, 2, "w1")
        gate_pass(blocks[0], 1, 3, "w1")
        load_x(2)
        quantize_w("wc", 1)
        empty_half(S, "c", 2, 0, turn_half("c", 2, 0))
        delay_x(1)
        interleave_w(V, "w0", 1, 0)
        interleave_w(S, "w0", 1, 1)
        load_w("w0", 0)
        delay_x(0)
        gate_pass(blocks[1], 1, 0, "w1")
        gate_pass(blocks[1], 1, 1, "w1")
        load_c(3)
        quantize_w("w0", 1)
        gate_pass(blocks[1], 1, 2, "w1")
        gate_pass(blocks[1], 1, 3, "w1")
        interleave_w(V, "wc", 0, 0)
        interleave_w(V, "w1", 0, 0)
        gate_pass(blocks[0], 1, 0, "wc")
        gate_pass(blocks[0], 1, 1, "wc")
        gate_pass(blocks[1], 1, 0, "wc")
        gate_pass(blocks[1], 1, 1, "wc")
        load_x(3)
        interleave_w(S, "wc", 0, 1)
        scale_x(2, 0)
        scale_x(2, 1)
        interleave_w(S, "w1", 0, 1)
        gate_pass(blocks[1], 1, 2, "wc")
        gate_pass(blocks[1], 1, 3, "wc")
        gate_pass(blocks[0], 1, 2, "wc")
        gate_pass(blocks[0], 1, 3, "wc")
        interleave_w(V, "w0", 0, 0)
        gate_pass(blocks[0], 1, 0, "w0")
        activate(blocks[0], 1, 0)
        gate_pass(blocks[0], 1, 1, "w0")
        activate(blocks[0], 1, 1)
        gate_pass(blocks[1], 1, 0, "w0")
        activate(blocks[1], 1, 0)
        gate_pass(blocks[1], 1, 1, "w0")
        activate(blocks[1], 1, 1)
        interleave_w(V, "w0", 0, 1)
        quantize_w("w1", 0)
        quantize_w("wc", 0)
        load_w("wk", 0)
        gate_pass(blocks[0], 1, 2, "w0")
        activate(blocks[0], 1, 2)
        gate_pass(blocks[0], 1, 3, "w0")
        activate(blocks[0], 1, 3)
        empty_half(S, "c", 2, 1, turn_half("c", 2, 1))
        empty_half(S, "c", 3, 0, turn_half("c", 3, 0))
        load_w("wk", 1)
        quantize_w("w0", 0)
        scale_x(2, 2)
        scale_x(2, 3)
        scale_x(3, 0)
        scale_x(3, 1)
        empty_half(S, "x", 2, 0, turn_half("x", 2, 0))
        gate_pass(blocks[1], 1, 2, "w0")
        activate(blocks[1], 1, 2)
        gate_pass(blocks[1], 1, 3, "w0")
        activate(blocks[1], 1, 3)
        interleave_w(V, "wk", 1, 0)
        empty_half(V, "c", 3, 1, turn_half("c", 3, 1))
        scale_x(3, 2)
        scale_x(3, 3)
        group(blocks[1], 0, 0)
        group(blocks[0], 0, 0)
        group(blocks[1], 0, 1)
        empty_half(S, "x", 2, 1, turn_half("x", 2, 1))
        empty_half(S, "x", 3, 0, turn_half("x", 3, 0))
        quantize_x(2)
        combine(blocks[0], 0)
        combine(blocks[1], 0)
        group(blocks[0], 0, 1)
        delay_x(2)
        combine(blocks[0], 1)
        interleave_w(S, "wk", 1, 1)
        group(blocks[0], 0, 2)
        quantize_c(2)
        empty_half(S, "x", 3, 1, turn_half("x", 3, 1))
        group(blocks[0], 0, 3)
        interleave_w(S, "wk", 0, 0)
        combine(blocks[0], 2)
        quantize_w("wk", 1)
        group(blocks[1], 0, 2)
        combine(blocks[0], 3)
        combine(blocks[1], 1)
        interleave_w(S, "wk", 0, 1)
        group(blocks[1], 0, 3)
        quantize_x(3)
        delay_x(3)
        interleave_z(blocks[0])
        group(blocks[2], 0, 0)
        group(blocks[2], 1, 0)
        quantize_w("wk", 0)
        group(blocks[2], 0, 1)
        quantize_z(blocks[0])
        combine(blocks[1], 2)
        group(blocks[2], 1, 1)
        group(blocks[2], 1, 2)
        combine(blocks[1], 3)
        second(blocks[0], 0, (V, S))
        second(blocks[0], 1, (S, S))
        interleave_z(blocks[1])
        second(blocks[0], 2, (S, S))
        second(blocks[0], 3, (V, V))
        quantize_z(blocks[1])
        group(blocks[2], 1, 3)
        quantize_c(3)
        group(blocks[2], 0, 2)
        group(blocks[2], 0, 3)
        combine(blocks[2], 0)
        second(blocks[1], 0, (S, S))
        combine(blocks[2], 1)
        combine(blocks[2], 2)
        second(blocks[1], 1, (S, S))
        combine(blocks[2], 3)
        group((3, 0, 256), 0, 0)
        group((3, 0, 256), 1, 0)
        interleave_z(blocks[2])
        group((3, 256, 512), 1, 0)
        second(blocks[1], 2, (V, S))
        group((3, 0, 256), 0, 1)
        quantize_z(blocks[2])
        group((3, 0, 256), 1, 1)
        combine((3, 0, 256), 0)
        second(blocks[1], 3, (V, S))
        group((3, 0, 256), 1, 2)
        group((3, 0, 256), 0, 2)
        group((3, 0, 256), 0, 3)
        combine((3, 0, 256), 1)
        second(blocks[2], 0, (V, V))
        group((3, 0, 256), 1, 3)
        combine((3, 0, 256), 2)
        group((3, 256, 512), 0, 0)
        second(blocks[2], 1, (S, S))
        combine((3, 0, 256), 3)
        group((3, 256, 512), 1, 1)
        interleave_z((3, 0, 256))
        group((3, 256, 512), 0, 1)
        second(blocks[2], 2, (S, V))
        group((3, 256, 512), 0, 2)
        quantize_z((3, 0, 256))
        second(blocks[2], 3, (V, S))
        combine((3, 256, 512), 0)
        group((3, 256, 512), 1, 2)
        group((3, 256, 512), 1, 3)
        group((3, 256, 512), 0, 3)
        combine((3, 256, 512), 1)
        second((3, 0, 256), 0, (S, S))
        combine((3, 256, 512), 2)
        combine((3, 256, 512), 3)
        interleave_z((3, 256, 512))
        second((3, 0, 256), 1, (S, S))
        quantize_z((3, 256, 512))
        second((3, 256, 512), 0, (S, S))
        second((3, 256, 512), 1, (S, V))
